import numpy as np
import ml_dtypes


def mxq(x, axis, fmt="e4m3"):
    dtype, down = {"e4m3": (ml_dtypes.float8_e4m3fn, 7), "e5m2": (ml_dtypes.float8_e5m2, 14)}[fmt]
    v = np.moveaxis(np.asarray(x, np.float32).astype(ml_dtypes.bfloat16).astype(np.float64), axis, -1)
    blocks = v.reshape(v.shape[:-1] + (-1, 32))
    amax = np.abs(blocks).max(-1, keepdims=True)
    byte = np.maximum(np.where(amax > 0, np.frexp(amax)[1] - 1 + 127, 0) - down, 1)
    scale = np.exp2(byte - 127.0)
    codes = (blocks / scale).astype(np.float32).astype(dtype).astype(np.float64)
    return np.moveaxis((codes * scale).reshape(v.shape), -1, axis)


WIDE = False


def mx_kscale(k):
    if not WIDE:
        return np.ones(k)
    levels = np.array([10, -10, 5, -5, 0])
    if k % 512:
        return np.exp2(np.random.permutation(np.resize(levels, k // 32))).repeat(32)
    a = np.empty((k // 512, 16))
    for p in range(k // 512):
        a[p, :8] = np.random.permutation(np.resize(levels, 8))
        for g in range(8):
            far = levels[np.abs(levels - a[p, g]) >= 10]
            a[p, g + 8] = far[np.random.randint(len(far))]
    return np.exp2(a.ravel()).repeat(32)


BF16 = ml_dtypes.bfloat16


def bf(x):
    return np.asarray(x, np.float32).astype(BF16)


def f64(x):
    return np.asarray(x).astype(np.float64)


E2M1 = np.array([0.0, 0.5, 1.0, 1.5, 2.0, 3.0, 4.0, 6.0, -0.0, -0.5, -1.0, -1.5, -2.0, -3.0, -4.0, -6.0])


def pack_weight(w, fmt):
    k, n = w.shape
    w = f64(bf(w)).reshape(k // 32, 32, n)
    amax = np.abs(w).max(1)
    if fmt == "e4m3":
        byte = np.frexp(amax)[1] - 1 + 127 - 7
    else:
        mant, ex = np.frexp(amax / 6.0)
        byte = np.where(mant > 0.5, ex, ex - 1) + 127
    byte = np.clip(np.where(amax > 0, byte, 1), 1, 254)
    scaled = (w * np.exp2(127.0 - byte)[:, None, :]).reshape(k, n).astype(np.float32)
    by_word = np.ascontiguousarray(scaled.reshape(k // 512, 128, 4, n).transpose(0, 1, 3, 2))
    if fmt == "e4m3":
        words = by_word.astype(ml_dtypes.float8_e4m3fn).view(np.uint8)
    else:
        c = by_word.astype(ml_dtypes.float4_e2m1fn).view(np.uint8) & 0xF
        words = c[..., 0::2] | (c[..., 1::2] << 4)
    return np.ascontiguousarray(words), np.ascontiguousarray(byte.astype(np.uint8).reshape(k // 512, 16, n))


def unpack_weight(words, scales, fmt):
    g, p, n, _ = words.shape
    if fmt == "e4m3":
        vals = np.ascontiguousarray(words).view(ml_dtypes.float8_e4m3fn).astype(np.float64)
    else:
        nib = np.empty((g, p, n, 4), np.uint8)
        nib[..., 0::2] = words & 0xF
        nib[..., 1::2] = words >> 4
        vals = E2M1[nib]
    vals = vals * np.repeat(np.exp2(scales.astype(np.float64) - 127.0), 8, axis=1)[..., None]
    return vals.transpose(0, 1, 3, 2).reshape(g * 512, n)
def pack4(w):
    words, scales = pack_weight(w, "e2m1")
    return words.reshape(words.shape[0], 128, -1), scales


def unpack4(words, scales):
    return unpack_weight(words.reshape(words.shape[0], 128, -1, 2), scales, "e2m1")


E4M3FN = np.array([(-1.0 if i & 128 else 1.0) * ((1.0 + (i & 7) / 8.0) * 2.0 ** (((i >> 3) & 15) - 7) if i & 120 else (i & 7) * 2.0 ** -9) for i in range(256)])


def e4m3fn_bytes(y):
    return np.clip(np.asarray(y, np.float64), -448.0, 448.0).astype(np.float32).astype(ml_dtypes.float8_e4m3fn).view(np.uint8)


def e4m3fn_values(b):
    return E4M3FN[b]


N, M, K = 1024, 1024, 1024


def soft_threshold(v, thr):
    return np.maximum(v - thr, 0.0) - np.maximum(-v - thr, 0.0)


def draw0():
    s, t = mx_kscale(M), mx_kscale(K)
    y = np.random.standard_normal((N, M)) * s
    a = np.random.standard_normal((M, K)) / np.sqrt(M) / s[:, None]
    g = (1.0 + 0.1 * np.random.standard_normal(K)) * t
    minv = np.random.standard_normal((K, K)) / np.sqrt(K) / t[:, None]
    z0 = np.random.standard_normal((N, K)) * 0.5
    u0 = np.random.standard_normal((N, K)) * 0.3
    lam = np.random.uniform(0.2, 0.6, K)
    a_words, a_scales = pack4(a)
    minv_words, minv_scales = pack4(minv)
    return {"y": bf(y), "a_words": a_words, "a_scales": a_scales, "g": bf(g), "minv_words": minv_words, "minv_scales": minv_scales, "z0": bf(z0), "u0": bf(u0), "lam": bf(lam)}


def core(y, a_words, a_scales, g, minv_words, minv_scales, z0, u0, lam):
    z0, u0 = f64(z0), f64(u0)
    q = mxq(f64(y), 1, "e4m3") @ unpack4(a_words, a_scales)
    r = f64(g)[None, :] * (q + 0.8 * (z0 - u0))
    x1 = mxq(r, 1, "e4m3") @ unpack4(minv_words, minv_scales)
    v = 1.6 * x1 - 0.6 * z0 + u0
    thr = (f64(lam) / 0.8)[None, :]
    z1 = soft_threshold(v, thr)
    u1 = v - z1
    return z1, u1


def setup_inputs():
    drawn = draw0()
    full = np.asarray(drawn['y']).astype(np.float64)
    scale = (np.abs(full).reshape(8, 128, 8, 128).max(axis=(1, 3)) / 448.0).astype(np.float32)
    given = {}
    for key, value in drawn.items():
        if key == 'y':
            given['y_bytes'] = e4m3fn_bytes(full / np.repeat(np.repeat(scale.astype(np.float64), 128, axis=0), 128, axis=1))
            given['y_scale'] = scale
        else:
            given[key] = value
    return given


def reference(y_bytes, y_scale, a_words, a_scales, g, minv_words, minv_scales, z0, u0, lam):
    return core(e4m3fn_values(y_bytes) * np.repeat(np.repeat(y_scale.astype(np.float64), 128, axis=0), 128, axis=1), a_words, a_scales, g, minv_words, minv_scales, z0, u0, lam)

@@ -1,0 +1,299 @@
+from contextlib import ExitStack
+
+import concourse.mybir as mybir
+from concourse.masks import make_identity
+
+F32 = mybir.dt.float32
+BF16 = mybir.dt.bfloat16
+I32 = mybir.dt.int32
+U32 = mybir.dt.uint32
+U8 = mybir.dt.uint8
+FP8 = mybir.dt.float8_e4m3fn
+FP8X4 = mybir.dt.float8_e4m3fn_x4
+FP4X4 = mybir.dt.float4_e2m1fn_x4
+ALU = mybir.AluOpType
+COPY = mybir.ActivationFunctionType.Copy
+
+N, M, K = 1024, 1024, 1024
+FLOPS = 2 * N * M * K + 2 * N * K * K
+P = 128
+TILES = N // P
+HALF = 512
+PASSES = 2
+
+ORDER = [("v0", 7),("widen", 1),("t0", 8),("W1", 4),("rc", 5),("e1", 9),("o0", 10),("z1", 11),("e0", 8),("b1", 10),("W0", 3),("yT", 1),("r", 4),("o1", 10),("d", 1),("k0", 9),("x1", 7),("qr", 5),("q0", 2),("z0", 10),("c1", 4),("yc", 1),("x0", 6),("s0", 2),("qy", 1),("q1", 2),("rT", 4),("k1", 9),("c0", 3),("t1", 8),("s1", 2),("v1", 7),("b0", 9)]
+PRE = [("widen", 0),("d", 0),("yT", 0),("yc", 0),("c0", 0),("qy", 0),("c1", 0),("widen", 1),("C0", 0),("d", 1),("C1", 0)]
+BANK = {"yT0":3,"q0":0,"q1":7,"rT0":2,"W0":4,"W1":1,"x0":6,"x1":5,"vT0":3,"vT1":4,"uT0":0,"uT1":2}
+DEPTH = {"ybf":2,"yg":2,"yq":3,"ys":3,"d":3,"s":3,"rb":2,"rg":2,"rq":3,"rs":3,"w":6,"v":6,"vt":3,"ut":2,"u1":4,"z1":3}
+D_ON_GPSIMD = []
+W_ON_VECTOR = [0,1]
+Z_FROM_PSUM = False
+
+
+def tile_unrolledoverrelaxedadmmlasso_d2p_kernel(
+    tc, y_bytes, y_scale, a_words, a_scales, g, minv_words, minv_scales, z0, u0, lam, out_0, out_1
+):
+    nc = tc.nc
+    with ExitStack() as ctx:
+        keep = ctx.enter_context(tc.tile_pool(name="keep", bufs=1))
+        psum = ctx.enter_context(tc.psum_pool(name="psum", bufs=1))
+        ctx.enter_context(tc.manual_schedule())
+
+        def ring(name, width, dtype):
+            return [
+                keep.tile([P, width], dtype, name="%s_%d" % (name, j), align_bytes=64) for j in range(DEPTH[name])
+            ]
+
+        banks = [psum.tile([P, HALF], F32, name="bank_%d" % j) for j in range(8)]
+        y_raw = keep.tile([P, TILES, M], U8, name="y_raw", align_bytes=64)
+        y_sc = keep.tile([P, TILES * TILES], F32, name="y_sc", align_bytes=64)
+        z_sb = keep.tile([P, TILES, K], BF16, name="z_sb", align_bytes=64)
+        u_sb = keep.tile([P, TILES, K], BF16, name="u_sb", align_bytes=64)
+        a_sb = keep.tile([P, PASSES, 2 * K], U8, name="a_sb", align_bytes=64)
+        m_sb = keep.tile([P, PASSES, 2 * K], U8, name="m_sb", align_bytes=64)
+        a_pl = keep.tile([P, PASSES, K], U8, name="a_pl", align_bytes=64)
+        m_pl = keep.tile([P, PASSES, K], U8, name="m_pl", align_bytes=64)
+        ident_f = keep.tile([P, P], F32, name="ident_f", align_bytes=64)
+        ident_b = keep.tile([P, P], BF16, name="ident_b", align_bytes=64)
+        diag_u = keep.tile([P, P], BF16, name="diag_u", align_bytes=64)
+        diag_z = keep.tile([P, P], BF16, name="diag_z", align_bytes=64)
+        rows = keep.tile([P, P], BF16, name="rows", align_bytes=64)
+        cols = keep.tile([P, 16], BF16, name="cols", align_bytes=64)
+        thr = keep.tile([P, 8], F32, name="thr", align_bytes=64)
+        neg_thr = keep.tile([P, 8], F32, name="neg_thr", align_bytes=64)
+        hi = keep.tile([P, 8], F32, name="hi", align_bytes=64)
+        lo = keep.tile([P, 8], F32, name="lo", align_bytes=64)
+        twice = keep.tile([P, 8], F32, name="twice", align_bytes=64)
+        sgn = keep.tile([P, 8], F32, name="sgn", align_bytes=64)
+        g_all = keep.tile([P, K], BF16, name="g_all", align_bytes=64)
+        warm = keep.tile([P, 8], F32, name="warm", align_bytes=64)
+
+        ybf = ring("ybf", M, BF16)
+        yg = ring("yg", M, BF16)
+        yq = ring("yq", M // 4, U32)
+        ys = ring("ys", M // 4, U8)
+        d = ring("d", K, F32)
+        s = ring("s", K, F32)
+        rb = ring("rb", K, BF16)
+        rg = ring("rg", K, BF16)
+        rq = ring("rq", K // 4, U32)
+        rs = ring("rs", K // 4, U8)
+        w = ring("w", K, F32)
+        v = ring("v", K, F32)
+        vt = ring("vt", K, F32)
+        ut = ring("ut", K, F32)
+        u1 = ring("u1", K, F32)
+        z1 = ring("z1", K, F32)
+
+        def at(tiles, i):
+            return tiles[i % len(tiles)]
+
+        def load_rows(dst, src, first, count):
+            nc.sync.dma_start(
+                out=dst[:, first : first + count, :],
+                in_=src[first * P : (first + count) * P, :].rearrange("(t p) k -> p t k", p=P),
+            )
+
+        def load_words(dst, src):
+            nc.sync.dma_start(out=dst[:].bitcast(I32), in_=src.rearrange("g p n -> p g n").bitcast(I32))
+
+        def load_plane(dst, src):
+            for q in range(4):
+                nc.gpsimd.dma_start(
+                    out=dst[32 * q : 32 * q + 4, :, :].bitcast(I32),
+                    in_=src[:, 4 * q : 4 * q + 4, :].rearrange("g r n -> r g n").bitcast(I32),
+                )
+
+        nc.gpsimd.memset(warm[:], 0.0)
+        nc.gpsimd.memset(a_pl[:].bitcast(I32), 0)
+        make_identity(nc, ident_f[:])
+        nc.gpsimd.memset(rows[:], 0.0)
+        make_identity(nc, ident_b[:])
+        load_plane(a_pl, a_scales)
+        nc.gpsimd.memset(m_pl[:].bitcast(I32), 0)
+        load_plane(m_pl, minv_scales)
+        nc.scalar.activation(out=warm[:, 4:5], in_=warm[:, 0:1], func=COPY, scale=2.0)
+
+        load_rows(y_raw, y_bytes, 0, 1)
+        nc.sync.dma_start(out=y_sc[:], in_=y_scale.rearrange("a b -> (a b)").partition_broadcast(P))
+        load_rows(z_sb, z0, 0, 1)
+        load_rows(u_sb, u0, 0, 1)
+        load_words(a_sb, a_words)
+        load_rows(z_sb, z0, 1, 1)
+        load_rows(u_sb, u0, 1, 1)
+        load_rows(y_raw, y_bytes, 1, 1)
+        nc.sync.dma_start(out=rows[0:8, :], in_=lam.rearrange("(b p) -> b p", p=P))
+        nc.sync.dma_start(out=rows[8:16, :], in_=g.rearrange("(b p) -> b p", p=P))
+        load_rows(y_raw, y_bytes, 2, 2)
+        load_rows(z_sb, z0, 2, 2)
+        load_rows(u_sb, u0, 2, 2)
+        load_words(m_sb, minv_words)
+        load_rows(y_raw, y_bytes, 4, 4)
+        for first in (4, 6):
+            load_rows(z_sb, z0, first, 2)
+            load_rows(u_sb, u0, first, 2)
+
+        def columns(i):
+            view = banks[7][:].bitcast(BF16)
+            nc.tensor.transpose(view[:, 0:P], rows[:], ident_b[:])
+            nc.vector.tensor_copy(out=cols[:], in_=view[:, 0:16])
+            nc.vector.tensor_scalar(out=diag_u[:], in0=ident_b[:], scalar1=5.0, scalar2=None, op0=ALU.mult)
+            nc.vector.tensor_scalar(out=diag_z[:], in0=ident_b[:], scalar1=-3.0, scalar2=None, op0=ALU.mult)
+            nc.vector.tensor_scalar(out=thr[:], in0=cols[:, 0:8], scalar1=1.25, scalar2=None, op0=ALU.mult)
+            nc.vector.tensor_scalar(out=neg_thr[:], in0=cols[:, 0:8], scalar1=-1.25, scalar2=None, op0=ALU.mult)
+            nc.vector.tensor_scalar(
+                out=twice[:], in0=cols[:, 0:8], scalar1=0.0, scalar2=2.0, op0=ALU.is_ge, op1=ALU.mult
+            )
+            nc.vector.tensor_tensor(out=hi[:], in0=thr[:], in1=neg_thr[:], op=ALU.max)
+            nc.vector.tensor_tensor(out=lo[:], in0=thr[:], in1=neg_thr[:], op=ALU.min)
+            nc.vector.tensor_scalar(out=sgn[:], in0=twice[:], scalar1=-1.0, scalar2=None, op0=ALU.add)
+
+        def spread_gain(i):
+            view = banks[6][:].bitcast(BF16)
+            for b in range(8):
+                nc.tensor.transpose(
+                    view[:, b * P : (b + 1) * P], cols[:, 8 + b : 9 + b].to_broadcast([P, P]), ident_b[:]
+                )
+            nc.scalar.copy(out=g_all[:], in_=view)
+
+        def widen(i):
+            for j in range(TILES):
+                nc.scalar.activation(
+                    out=at(ybf, i)[:, j * P : (j + 1) * P],
+                    in_=y_raw[:, i, j * P : (j + 1) * P].bitcast(FP8),
+                    func=COPY,
+                    scale=y_sc[:, i * TILES + j : i * TILES + j + 1],
+                )
+
+        def turn_words(src, bank):
+            words = src[:].bitcast(F32)
+            for c in range(PASSES):
+                for e in range(2):
+                    nc.tensor.transpose(
+                        bank[:, (2 * c + e) * P : (2 * c + e + 1) * P],
+                        words[:, 256 * c + e : 256 * (c + 1) : 2],
+                        ident_f[:],
+                    )
+
+        def group_words(bank, dst):
+            nc.scalar.copy(
+                out=dst[:].bitcast(F32).rearrange("p (c r e) -> p c r e", c=PASSES, e=2),
+                in_=bank[:].rearrange("p (c e r) -> p c r e", c=PASSES, e=2),
+            )
+
+        def quantize(src, codes, scales):
+            nc.vector.quantize_mx(out=codes[:].bitcast(FP8X4), scales=scales[:], in_=src[:])
+
+        def product(bank, codes, scales, words, plane, h):
+            for c in range(PASSES):
+                nc.tensor.matmul_mx(
+                    out=bank[:],
+                    lhsT=codes[:, c * P : (c + 1) * P].bitcast(FP8X4),
+                    lhsT_scale=scales[:, c * P : (c + 1) * P],
+                    rhs=words[:, c, 2 * HALF * h : 2 * HALF * (h + 1)].bitcast(FP4X4),
+                    rhs_scale=plane[:, c, HALF * h : HALF * (h + 1)],
+                    start=(c == 0),
+                    stop=(c == PASSES - 1),
+                )
+
+        def half(h):
+            return slice(HALF * h, HALF * (h + 1))
+
+        def turn_blocks(src, bank, h):
+            for b in range(4):
+                nc.tensor.transpose(
+                    bank[:, b * P : (b + 1) * P], src[:, HALF * h + b * P : HALF * h + (b + 1) * P], ident_f[:]
+                )
+
+        def stage(name, i):
+            kind = name[0]
+            h = int(name[1]) if name[1:] in ("0", "1") else 0
+            rows_i = slice(i * P, (i + 1) * P)
+            if name == "C0":
+                columns(i)
+            elif name == "C1":
+                spread_gain(i)
+            elif name == "widen":
+                widen(i)
+            elif name == "yT":
+                turn_words(at(ybf, i), banks[BANK["yT0"]])
+            elif name == "yc":
+                group_words(banks[BANK["yT0"]], at(yg, i))
+            elif name == "qy":
+                quantize(at(yg, i), at(yq, i), at(ys, i))
+            elif name == "d":
+                eng = nc.gpsimd if i in D_ON_GPSIMD else nc.vector
+                eng.tensor_tensor(out=at(d, i)[:], in0=z_sb[:, i, :], in1=u_sb[:, i, :], op=ALU.subtract)
+            elif name == "r":
+                nc.vector.tensor_tensor(out=at(rb, i)[:], in0=at(s, i)[:], in1=g_all[:], op=ALU.mult)
+            elif name == "rT":
+                turn_words(at(rb, i), banks[BANK["rT0"]])
+            elif name == "rc":
+                group_words(banks[BANK["rT0"]], at(rg, i))
+            elif name == "qr":
+                quantize(at(rg, i), at(rq, i), at(rs, i))
+            elif kind == "q":
+                product(banks[BANK["q%d" % h]], at(yq, i), at(ys, i), a_sb, a_pl, h)
+            elif kind == "s":
+                nc.vector.scalar_tensor_tensor(
+                    out=at(s, i)[:, half(h)], in0=at(d, i)[:, half(h)], scalar=0.8,
+                    in1=banks[BANK["q%d" % h]][:], op0=ALU.mult, op1=ALU.add,
+                )
+            elif kind == "W":
+                if i not in W_ON_VECTOR:
+                    bank = banks[BANK["W%d" % h]]
+                    nc.tensor.matmul(bank[:], lhsT=diag_u[:], rhs=u_sb[:, i, half(h)], start=True, stop=False)
+                    nc.tensor.matmul(bank[:], lhsT=diag_z[:], rhs=z_sb[:, i, half(h)], start=False, stop=True)
+            elif kind == "c":
+                if i not in W_ON_VECTOR:
+                    nc.scalar.activation(
+                        out=at(w, i)[:, half(h)], in_=banks[BANK["W%d" % h]][:], func=COPY, scale=0.2
+                    )
+                else:
+                    nc.vector.scalar_tensor_tensor(
+                        out=at(w, i)[:, half(h)], in0=z_sb[:, i, half(h)], scalar=-0.6,
+                        in1=u_sb[:, i, half(h)], op0=ALU.mult, op1=ALU.add,
+                    )
+            elif kind == "x":
+                product(banks[BANK["x%d" % h]], at(rq, i), at(rs, i), m_sb, m_pl, h)
+            elif kind == "v":
+                nc.vector.scalar_tensor_tensor(
+                    out=at(v, i)[:, half(h)], in0=banks[BANK["x%d" % h]][:], scalar=1.6,
+                    in1=at(w, i)[:, half(h)], op0=ALU.mult, op1=ALU.add,
+                )
+            elif kind == "t":
+                turn_blocks(at(v, i), banks[BANK["vT%d" % h]], h)
+            elif kind == "e":
+                for b in range(4):
+                    j = 4 * h + b
+                    nc.scalar.activation(
+                        out=at(vt, i)[:, j * P : (j + 1) * P],
+                        in_=banks[BANK["vT%d" % h]][:, b * P : (b + 1) * P],
+                        func=COPY,
+                        scale=sgn[:, j : j + 1],
+                    )
+            elif kind == "k":
+                for j in range(4 * h, 4 * h + 4):
+                    nc.vector.tensor_scalar(
+                        out=at(ut, i)[:, j * P : (j + 1) * P], in0=at(vt, i)[:, j * P : (j + 1) * P],
+                        scalar1=hi[:, j : j + 1], scalar2=lo[:, j : j + 1], op0=ALU.min, op1=ALU.max,
+                    )
+            elif kind == "b":
+                turn_blocks(at(ut, i), banks[BANK["uT%d" % h]], h)
+            elif kind == "o":
+                nc.scalar.copy(out=at(u1, i)[:, half(h)], in_=banks[BANK["uT%d" % h]][:])
+                nc.sync.dma_start(out=out_1[rows_i, half(h)], in_=at(u1, i)[:, half(h)])
+            elif kind == "z":
+                dual = banks[BANK["uT%d" % h]][:] if Z_FROM_PSUM else at(u1, i)[:, half(h)]
+                nc.vector.tensor_tensor(
+                    out=at(z1, i)[:, half(h)], in0=at(v, i)[:, half(h)], in1=dual, op=ALU.subtract
+                )
+                nc.sync.dma_start(out=out_0[rows_i, half(h)], in_=at(z1, i)[:, half(h)])
+
+        for name, i in PRE:
+            stage(name, i)
+        for step in range(TILES + max(lag for name, lag in ORDER)):
+            for name, lag in ORDER:
+                i = step - lag
+                if 0 <= i < TILES and (name, i) not in PRE:
+                    stage(name, i)

@@ -12,7 +12,8 @@ FP8 = mybir.dt.float8_e4m3fn
 FP8X4 = mybir.dt.float8_e4m3fn_x4
 FP4X4 = mybir.dt.float4_e2m1fn_x4
 ALU = mybir.AluOpType
-COPY = mybir.ActivationFunctionType.Copy
+ACT = mybir.ActivationFunctionType
+COPY = ACT.Copy
 
 N, M, K = 1024, 1024, 1024
 FLOPS = 2 * N * M * K + 2 * N * K * K
@@ -21,12 +22,12 @@ TILES = N // P
 HALF = 512
 PASSES = 2
 
-ORDER = [("v0", 7),("widen", 1),("t0", 8),("W1", 4),("rc", 5),("e1", 9),("o0", 10),("z1", 11),("e0", 8),("b1", 10),("W0", 3),("yT", 1),("r", 4),("o1", 10),("d", 1),("k0", 9),("x1", 7),("qr", 5),("q0", 2),("z0", 10),("c1", 4),("yc", 1),("x0", 6),("s0", 2),("qy", 1),("q1", 2),("rT", 4),("k1", 9),("c0", 3),("t1", 8),("s1", 2),("v1", 7),("b0", 9)]
-PRE = [("widen", 0),("d", 0),("yT", 0),("yc", 0),("c0", 0),("qy", 0),("c1", 0),("widen", 1),("C0", 0),("d", 1),("C1", 0)]
-BANK = {"yT0":3,"q0":0,"q1":7,"rT0":2,"W0":4,"W1":1,"x0":6,"x1":5,"vT0":3,"vT1":4,"uT0":0,"uT1":2}
-DEPTH = {"ybf":2,"yg":2,"yq":3,"ys":3,"d":3,"s":3,"rb":2,"rg":2,"rq":3,"rs":3,"w":6,"v":6,"vt":3,"ut":2,"u1":4,"z1":3}
+SEQ = [("widen", 0, -1), ("yT", 0, 0), ("c1", 0, -1), ("d", 0, -1), ("yc", 0, -1), ("qy", 0, -1), ("c0", 0, -1), ("C0a", 0, 1), ("q0", 0, 2), ("C0", 0, -1), ("c1", 1, -1), ("C1a", 0, 3), ("widen", 1, -1), ("s0", 0, -1), ("d", 1, -1), ("q1", 0, 4), ("C1", 0, -1), ("yT", 1, 5), ("widen", 2, -1), ("s1", 0, -1), ("W0", 2, 6), ("c0", 1, -1), ("W1", 2, 7), ("r", 0, -1), ("yc", 1, -1), ("yT", 2, 0), ("widen", 3, -1), ("qy", 1, -1), ("rT", 0, 1), ("d", 2, -1), ("q1", 1, 2), ("yc", 2, -1), ("d", 3, -1), ("rc", 0, -1), ("yT", 3, 3), ("c1", 2, -1), ("q0", 1, 4), ("qr", 0, -1), ("yc", 3, -1), ("s1", 1, -1), ("x1", 0, 5), ("c0", 2, -1), ("s0", 1, -1), ("x0", 0, 0), ("widen", 4, -1), ("v1", 0, -1), ("W0", 5, 1), ("qy", 3, -1), ("t1", 0, 7), ("qy", 2, -1), ("widen", 5, -1), ("yT", 4, 3), ("r", 1, -1), ("q1", 2, 2), ("v0", 0, -1), ("e1", 0, -1), ("q0", 2, 6), ("s1", 2, -1), ("widen", 7, -1), ("t0", 0, 4), ("rT", 1, 5), ("s0", 2, -1), ("k1", 0, -1), ("W1", 4, 0), ("r", 2, -1), ("e0", 0, -1), ("b1", 0, 7), ("W1", 7, 2), ("c1", 4, -1), ("k0", 0, -1), ("o1", 0, -1), ("rT", 2, 6), ("d", 5, -1), ("b0", 0, 4), ("rc", 1, -1), ("q1", 3, 0), ("rc", 2, -1), ("z1", 0, -1), ("yc", 4, -1), ("yT", 5, 7), ("s1", 3, -1), ("o0", 0, -1), ("q0", 3, 5), ("qr", 2, -1), ("qr", 1, -1), ("yc", 5, -1), ("x0", 2, 6), ("z0", 0, -1), ("widen", 6, -1), ("x0", 1, 3), ("s0", 3, -1), ("x1", 1, 0), ("v0", 2, -1), ("x1", 2, 4), ("v0", 1, -1), ("r", 3, -1), ("yT", 6, 7), ("t0", 1, 5), ("yc", 6, -1), ("W1", 6, 6), ("v1", 2, -1), ("c0", 5, -1), ("rT", 3, 3), ("v1", 1, -1), ("e0", 1, -1), ("t1", 2, 7), ("qy", 6, -1), ("t1", 1, 4), ("qy", 4, -1), ("rc", 3, -1), ("d", 4, -1), ("q1", 6, 1), ("e1", 1, -1), ("q1", 4, 0), ("qr", 3, -1), ("c1", 6, -1), ("q0", 4, 5), ("k1", 1, -1), ("e1", 2, -1), ("s1", 4, -1), ("x1", 3, 3), ("x0", 3, 4), ("s0", 4, -1), ("v1", 3, -1), ("q0", 6, 6), ("k1", 2, -1), ("v0", 3, -1), ("r", 4, -1), ("b1", 1, 0), ("t0", 3, 7), ("o1", 1, -1), ("qy", 5, -1), ("k0", 1, -1), ("rT", 4, 5), ("z1", 1, -1), ("y0", 3, -1), ("b0", 1, 3), ("d", 6, -1), ("rc", 4, -1), ("q1", 5, 4), ("o0", 1, -1), ("q0", 5, 0), ("qr", 4, -1), ("e0", 3, -1), ("s1", 5, -1), ("x1", 4, 5), ("s0", 5, -1), ("W0", 4, 3), ("k0", 3, -1), ("t1", 3, 4), ("r", 5, -1), ("c0", 4, -1), ("b0", 3, 7), ("s0", 6, -1), ("y1", 3, -1), ("a0", 3, 0), ("s1", 6, -1), ("c1", 7, -1), ("W1", 5, 3), ("v1", 4, -1), ("z0", 3, -1), ("W0", 6, 6), ("r", 6, -1), ("c1", 5, -1), ("yT", 7, 1), ("e1", 3, -1), ("t1", 4, 2), ("d", 7, -1), ("t0", 2, 5), ("yc", 7, -1), ("rT", 5, 0), ("c0", 6, -1), ("qy", 7, -1), ("W0", 7, 3), ("z0", 1, -1), ("e1", 4, -1), ("q1", 7, 4), ("k1", 3, -1), ("c0", 7, -1), ("q0", 7, 1), ("k1", 4, -1), ("s1", 7, -1), ("e0", 2, -1), ("b1", 4, 6), ("s0", 7, -1), ("b1", 3, 2), ("rc", 5, -1), ("b1", 2, 3), ("k0", 2, -1), ("o1", 4, -1), ("x0", 4, 4), ("qr", 5, -1), ("r", 7, -1), ("o1", 3, -1), ("x0", 5, 5), ("o1", 2, -1), ("x1", 5, 1), ("v0", 4, -1), ("o0", 3, -1), ("b0", 2, 0), ("z1", 4, -1), ("t0", 4, 6), ("o0", 2, -1), ("rT", 7, 2), ("v0", 5, -1), ("e0", 4, -1), ("rT", 6, 3), ("z0", 2, -1), ("t0", 5, 4), ("v1", 5, -1), ("rc", 6, -1), ("a1", 3, 7), ("k0", 4, -1), ("rc", 7, -1), ("t1", 5, 0), ("qr", 6, -1), ("b0", 4, 5), ("z1", 2, -1), ("e0", 5, -1), ("x0", 6, 6), ("qr", 7, -1), ("e1", 5, -1), ("k0", 5, -1), ("x1", 7, 1), ("v0", 6, -1), ("z1", 3, -1), ("b0", 5, 3), ("v1", 7, -1), ("o0", 4, -1), ("t0", 6, 2), ("k1", 5, -1), ("x0", 7, 4), ("e0", 6, -1), ("z0", 4, -1), ("b1", 5, 0), ("v0", 7, -1), ("o0", 5, -1), ("t1", 7, 6), ("k0", 6, -1), ("o1", 5, -1), ("x1", 6, 7), ("z0", 5, -1), ("e1", 7, -1), ("b0", 6, 1), ("z1", 5, -1), ("t0", 7, 5), ("o0", 6, -1), ("k1", 7, -1), ("v1", 6, -1), ("e0", 7, -1), ("b1", 7, 2), ("z0", 6, -1), ("t1", 6, 4), ("o1", 7, -1), ("k0", 7, -1), ("e1", 6, -1), ("z1", 7, -1), ("b0", 7, 3), ("o0", 7, -1), ("k1", 6, -1), ("b1", 6, 0), ("z0", 7, -1), ("o1", 6, -1), ("z1", 6, -1)]
+DEPTH = {"ybf":3,"yg":3,"yq":3,"ys":3,"d":4,"s":3,"rb":3,"rg":3,"rq":3,"rs":3,"w":4,"v":5,"vt":3,"ut":3,"u1":5,"z1":5,"nv":1}
 D_ON_GPSIMD = []
 W_ON_VECTOR = [0,1]
+WIDEN_ON_VECTOR = [0]
+SUM_ON_TENSOR = [3]
 Z_FROM_PSUM = False
 
 
@@ -45,6 +46,13 @@ def tile_unrolledoverrelaxedadmmlasso_d2p_kernel(
             ]
 
         banks = [psum.tile([P, HALF], F32, name="bank_%d" % j) for j in range(8)]
+        held = {}
+
+        def bank_of(role, i, fresh=None):
+            if fresh is not None:
+                held[role, i] = banks[fresh]
+            return held[role, i]
+
         y_raw = keep.tile([P, TILES, M], U8, name="y_raw", align_bytes=64)
         y_sc = keep.tile([P, TILES * TILES], F32, name="y_sc", align_bytes=64)
         z_sb = keep.tile([P, TILES, K], BF16, name="z_sb", align_bytes=64)
@@ -58,12 +66,10 @@ def tile_unrolledoverrelaxedadmmlasso_d2p_kernel(
         diag_u = keep.tile([P, P], BF16, name="diag_u", align_bytes=64)
         diag_z = keep.tile([P, P], BF16, name="diag_z", align_bytes=64)
         rows = keep.tile([P, P], BF16, name="rows", align_bytes=64)
-        cols = keep.tile([P, 16], BF16, name="cols", align_bytes=64)
-        thr = keep.tile([P, 8], F32, name="thr", align_bytes=64)
-        neg_thr = keep.tile([P, 8], F32, name="neg_thr", align_bytes=64)
+        cols = keep.tile([P, 8], BF16, name="cols", align_bytes=64)
         hi = keep.tile([P, 8], F32, name="hi", align_bytes=64)
         lo = keep.tile([P, 8], F32, name="lo", align_bytes=64)
-        twice = keep.tile([P, 8], F32, name="twice", align_bytes=64)
+        sgn_fifth = keep.tile([P, 8], F32, name="sgn_fifth", align_bytes=64)
         sgn = keep.tile([P, 8], F32, name="sgn", align_bytes=64)
         g_all = keep.tile([P, K], BF16, name="g_all", align_bytes=64)
         warm = keep.tile([P, 8], F32, name="warm", align_bytes=64)
@@ -84,6 +90,7 @@ def tile_unrolledoverrelaxedadmmlasso_d2p_kernel(
         ut = ring("ut", K, F32)
         u1 = ring("u1", K, F32)
         z1 = ring("z1", K, F32)
+        nv = ring("nv", K, F32)
 
         def at(tiles, i):
             return tiles[i % len(tiles)]
@@ -97,73 +104,71 @@ def tile_unrolledoverrelaxedadmmlasso_d2p_kernel(
         def load_words(dst, src):
             nc.sync.dma_start(out=dst[:].bitcast(I32), in_=src.rearrange("g p n -> p g n").bitcast(I32))
 
-        def load_plane(dst, src):
+        def load_plane(queue, dst, src):
             for q in range(4):
-                nc.gpsimd.dma_start(
+                queue.dma_start(
                     out=dst[32 * q : 32 * q + 4, :, :].bitcast(I32),
                     in_=src[:, 4 * q : 4 * q + 4, :].rearrange("g r n -> r g n").bitcast(I32),
                 )
 
-        nc.gpsimd.memset(warm[:], 0.0)
-        nc.gpsimd.memset(a_pl[:].bitcast(I32), 0)
+        nc.vector.memset(warm[:], 0.0)
+        nc.vector.memset(a_pl[:].bitcast(I32), 0)
+        nc.vector.memset(rows[:], 0.0)
+        nc.vector.memset(m_pl[:].bitcast(I32), 0)
         make_identity(nc, ident_f[:])
-        nc.gpsimd.memset(rows[:], 0.0)
-        make_identity(nc, ident_b[:])
-        load_plane(a_pl, a_scales)
-        nc.gpsimd.memset(m_pl[:].bitcast(I32), 0)
-        load_plane(m_pl, minv_scales)
-        nc.scalar.activation(out=warm[:, 4:5], in_=warm[:, 0:1], func=COPY, scale=2.0)
+        nc.scalar.activation(out=warm[:, 4:5], in_=warm[:, 0:1], func=ACT.Sign)
+        nc.vector.tensor_copy(out=ident_b[:], in_=ident_f[:])
+        nc.vector.tensor_scalar(out=diag_u[:], in0=ident_f[:], scalar1=5.0, scalar2=None, op0=ALU.mult)
+        nc.vector.tensor_scalar(out=diag_z[:], in0=ident_f[:], scalar1=-3.0, scalar2=None, op0=ALU.mult)
 
         load_rows(y_raw, y_bytes, 0, 1)
         nc.sync.dma_start(out=y_sc[:], in_=y_scale.rearrange("a b -> (a b)").partition_broadcast(P))
         load_rows(z_sb, z0, 0, 1)
         load_rows(u_sb, u0, 0, 1)
+        load_plane(nc.sync, a_pl, a_scales)
         load_words(a_sb, a_words)
+        nc.sync.dma_start(out=rows[0:8, :], in_=lam.rearrange("(b p) -> b p", p=P))
+        nc.sync.dma_start(out=rows[8:16, :], in_=g.rearrange("(b p) -> b p", p=P))
         load_rows(z_sb, z0, 1, 1)
         load_rows(u_sb, u0, 1, 1)
         load_rows(y_raw, y_bytes, 1, 1)
-        nc.sync.dma_start(out=rows[0:8, :], in_=lam.rearrange("(b p) -> b p", p=P))
-        nc.sync.dma_start(out=rows[8:16, :], in_=g.rearrange("(b p) -> b p", p=P))
         load_rows(y_raw, y_bytes, 2, 2)
-        load_rows(z_sb, z0, 2, 2)
-        load_rows(u_sb, u0, 2, 2)
+        load_rows(z_sb, z0, 2, 1)
+        load_rows(u_sb, u0, 2, 1)
+        load_plane(nc.sync, m_pl, minv_scales)
         load_words(m_sb, minv_words)
+        load_rows(z_sb, z0, 3, 1)
+        load_rows(u_sb, u0, 3, 1)
         load_rows(y_raw, y_bytes, 4, 4)
-        for first in (4, 6):
-            load_rows(z_sb, z0, first, 2)
-            load_rows(u_sb, u0, first, 2)
+        load_rows(z_sb, z0, 4, 2)
+        load_rows(u_sb, u0, 4, 2)
+        load_rows(z_sb, z0, 6, 2)
+        load_rows(u_sb, u0, 6, 2)
 
         def columns(i):
-            view = banks[7][:].bitcast(BF16)
-            nc.tensor.transpose(view[:, 0:P], rows[:], ident_b[:])
-            nc.vector.tensor_copy(out=cols[:], in_=view[:, 0:16])
-            nc.vector.tensor_scalar(out=diag_u[:], in0=ident_b[:], scalar1=5.0, scalar2=None, op0=ALU.mult)
-            nc.vector.tensor_scalar(out=diag_z[:], in0=ident_b[:], scalar1=-3.0, scalar2=None, op0=ALU.mult)
-            nc.vector.tensor_scalar(out=thr[:], in0=cols[:, 0:8], scalar1=1.25, scalar2=None, op0=ALU.mult)
-            nc.vector.tensor_scalar(out=neg_thr[:], in0=cols[:, 0:8], scalar1=-1.25, scalar2=None, op0=ALU.mult)
-            nc.vector.tensor_scalar(
-                out=twice[:], in0=cols[:, 0:8], scalar1=0.0, scalar2=2.0, op0=ALU.is_ge, op1=ALU.mult
-            )
-            nc.vector.tensor_tensor(out=hi[:], in0=thr[:], in1=neg_thr[:], op=ALU.max)
-            nc.vector.tensor_tensor(out=lo[:], in0=thr[:], in1=neg_thr[:], op=ALU.min)
-            nc.vector.tensor_scalar(out=sgn[:], in0=twice[:], scalar1=-1.0, scalar2=None, op0=ALU.add)
+            view = bank_of("c", 0)[:].bitcast(BF16)
+            nc.scalar.copy(out=cols[:], in_=view[:, 8:16])
+            nc.scalar.activation(out=sgn[:], in_=view[:, 0:8], func=ACT.Sign)
+            nc.scalar.activation(out=hi[:], in_=view[:, 0:8], func=ACT.Abs, scale=1.25)
+            nc.scalar.activation(out=lo[:], in_=hi[:], func=COPY, scale=-1.0)
+            nc.scalar.activation(out=sgn_fifth[:], in_=sgn[:], func=COPY, scale=0.2)
 
-        def spread_gain(i):
-            view = banks[6][:].bitcast(BF16)
+        def spread_gain(bank_id):
+            view = bank_of("c", 1, bank_id)[:].bitcast(BF16)
             for b in range(8):
                 nc.tensor.transpose(
-                    view[:, b * P : (b + 1) * P], cols[:, 8 + b : 9 + b].to_broadcast([P, P]), ident_b[:]
+                    view[:, b * P : (b + 1) * P], cols[:, b : b + 1].to_broadcast([P, P]), ident_b[:]
                 )
-            nc.scalar.copy(out=g_all[:], in_=view)
 
         def widen(i):
             for j in range(TILES):
-                nc.scalar.activation(
-                    out=at(ybf, i)[:, j * P : (j + 1) * P],
-                    in_=y_raw[:, i, j * P : (j + 1) * P].bitcast(FP8),
-                    func=COPY,
-                    scale=y_sc[:, i * TILES + j : i * TILES + j + 1],
-                )
+                dst = at(ybf, i)[:, j * P : (j + 1) * P]
+                src = y_raw[:, i, j * P : (j + 1) * P].bitcast(FP8)
+                scale = y_sc[:, i * TILES + j : i * TILES + j + 1]
+                if i in WIDEN_ON_VECTOR:
+                    nc.vector.tensor_scalar(out=dst, in0=src, scalar1=scale, scalar2=None, op0=ALU.mult)
+                else:
+                    nc.scalar.activation(out=dst, in_=src, func=COPY, scale=scale)
 
         def turn_words(src, bank):
             words = src[:].bitcast(F32)
@@ -205,20 +210,24 @@ def tile_unrolledoverrelaxedadmmlasso_d2p_kernel(
                     bank[:, b * P : (b + 1) * P], src[:, HALF * h + b * P : HALF * h + (b + 1) * P], ident_f[:]
                 )
 
-        def stage(name, i):
+        def stage(name, i, bank_id):
             kind = name[0]
             h = int(name[1]) if name[1:] in ("0", "1") else 0
             rows_i = slice(i * P, (i + 1) * P)
             if name == "C0":
                 columns(i)
+            elif name == "C0a":
+                nc.tensor.transpose(bank_of("c", 0, bank_id)[:].bitcast(BF16)[:, 0:P], rows[:], ident_b[:])
+            elif name == "C1a":
+                spread_gain(bank_id)
             elif name == "C1":
-                spread_gain(i)
+                nc.scalar.copy(out=g_all[:], in_=bank_of("c", 1)[:].bitcast(BF16))
             elif name == "widen":
                 widen(i)
             elif name == "yT":
-                turn_words(at(ybf, i), banks[BANK["yT0"]])
+                turn_words(at(ybf, i), bank_of("yT0", i, bank_id))
             elif name == "yc":
-                group_words(banks[BANK["yT0"]], at(yg, i))
+                group_words(bank_of("yT0", i), at(yg, i))
             elif name == "qy":
                 quantize(at(yg, i), at(yq, i), at(ys, i))
             elif name == "d":
@@ -227,27 +236,27 @@ def tile_unrolledoverrelaxedadmmlasso_d2p_kernel(
             elif name == "r":
                 nc.vector.tensor_tensor(out=at(rb, i)[:], in0=at(s, i)[:], in1=g_all[:], op=ALU.mult)
             elif name == "rT":
-                turn_words(at(rb, i), banks[BANK["rT0"]])
+                turn_words(at(rb, i), bank_of("rT0", i, bank_id))
             elif name == "rc":
-                group_words(banks[BANK["rT0"]], at(rg, i))
+                group_words(bank_of("rT0", i), at(rg, i))
             elif name == "qr":
                 quantize(at(rg, i), at(rq, i), at(rs, i))
             elif kind == "q":
-                product(banks[BANK["q%d" % h]], at(yq, i), at(ys, i), a_sb, a_pl, h)
+                product(bank_of("q%d" % h, i, bank_id), at(yq, i), at(ys, i), a_sb, a_pl, h)
             elif kind == "s":
                 nc.vector.scalar_tensor_tensor(
                     out=at(s, i)[:, half(h)], in0=at(d, i)[:, half(h)], scalar=0.8,
-                    in1=banks[BANK["q%d" % h]][:], op0=ALU.mult, op1=ALU.add,
+                    in1=bank_of("q%d" % h, i)[:], op0=ALU.mult, op1=ALU.add,
                 )
             elif kind == "W":
-                if i not in W_ON_VECTOR:
-                    bank = banks[BANK["W%d" % h]]
+                if i not in W_ON_VECTOR and i not in SUM_ON_TENSOR:
+                    bank = bank_of("W%d" % h, i, bank_id)
                     nc.tensor.matmul(bank[:], lhsT=diag_u[:], rhs=u_sb[:, i, half(h)], start=True, stop=False)
                     nc.tensor.matmul(bank[:], lhsT=diag_z[:], rhs=z_sb[:, i, half(h)], start=False, stop=True)
             elif kind == "c":
                 if i not in W_ON_VECTOR:
                     nc.scalar.activation(
-                        out=at(w, i)[:, half(h)], in_=banks[BANK["W%d" % h]][:], func=COPY, scale=0.2
+                        out=at(w, i)[:, half(h)], in_=bank_of("W%d" % h, i)[:], func=COPY, scale=0.2
                     )
                 else:
                     nc.vector.scalar_tensor_tensor(
@@ -255,22 +264,63 @@ def tile_unrolledoverrelaxedadmmlasso_d2p_kernel(
                         in1=u_sb[:, i, half(h)], op0=ALU.mult, op1=ALU.add,
                     )
             elif kind == "x":
-                product(banks[BANK["x%d" % h]], at(rq, i), at(rs, i), m_sb, m_pl, h)
+                product(bank_of("x%d" % h, i, bank_id), at(rq, i), at(rs, i), m_sb, m_pl, h)
+            elif kind == "v" and i in SUM_ON_TENSOR:
+                nc.scalar.activation(
+                    out=at(v, i)[:, half(h)], in_=bank_of("x%d" % h, i)[:], func=COPY,
+                    scale=1.6 if i in W_ON_VECTOR else 8.0,
+                )
+            elif kind == "t" and i in SUM_ON_TENSOR:
+                bank = bank_of("vT%d" % h, i, bank_id)
+                for b in range(4):
+                    blk = slice(HALF * h + b * P, HALF * h + (b + 1) * P)
+                    dst = bank[:, b * P : (b + 1) * P]
+                    nc.tensor.matmul(
+                        dst, lhsT=at(v, i)[:, blk], rhs=ident_f[:], is_transpose=True, start=True, stop=False
+                    )
+                    if i in W_ON_VECTOR:
+                        nc.tensor.matmul(
+                            dst, lhsT=at(w, i)[:, blk], rhs=ident_f[:], is_transpose=True, start=False, stop=True
+                        )
+                    else:
+                        nc.tensor.matmul(dst, lhsT=u_sb[:, i, blk], rhs=diag_u[:], start=False, stop=False)
+                        nc.tensor.matmul(dst, lhsT=z_sb[:, i, blk], rhs=diag_z[:], start=False, stop=True)
+            elif kind == "y":
+                nc.scalar.activation(
+                    out=at(nv, i)[:, half(h)], in_=bank_of("vT%d" % h, i)[:], func=COPY,
+                    scale=-1.0 if i in W_ON_VECTOR else -0.2,
+                )
+            elif kind == "a":
+                bank = bank_of("zT%d" % h, i, bank_id)
+                for b in range(4):
+                    blk = slice(HALF * h + b * P, HALF * h + (b + 1) * P)
+                    dst = bank[:, b * P : (b + 1) * P]
+                    nc.tensor.matmul(
+                        dst, lhsT=at(ut, i)[:, blk], rhs=ident_f[:], is_transpose=True, start=True, stop=False
+                    )
+                    nc.tensor.matmul(
+                        dst, lhsT=at(nv, i)[:, blk], rhs=ident_f[:], is_transpose=True, start=False, stop=True
+                    )
+            elif kind == "z" and i in SUM_ON_TENSOR:
+                nc.scalar.activation(
+                    out=at(z1, i)[:, half(h)], in_=bank_of("zT%d" % h, i)[:], func=COPY, scale=-1.0
+                )
+                nc.sync.dma_start(out=out_0[rows_i, half(h)], in_=at(z1, i)[:, half(h)])
             elif kind == "v":
                 nc.vector.scalar_tensor_tensor(
-                    out=at(v, i)[:, half(h)], in0=banks[BANK["x%d" % h]][:], scalar=1.6,
+                    out=at(v, i)[:, half(h)], in0=bank_of("x%d" % h, i)[:], scalar=1.6,
                     in1=at(w, i)[:, half(h)], op0=ALU.mult, op1=ALU.add,
                 )
             elif kind == "t":
-                turn_blocks(at(v, i), banks[BANK["vT%d" % h]], h)
+                turn_blocks(at(v, i), bank_of("vT%d" % h, i, bank_id), h)
             elif kind == "e":
                 for b in range(4):
                     j = 4 * h + b
                     nc.scalar.activation(
                         out=at(vt, i)[:, j * P : (j + 1) * P],
-                        in_=banks[BANK["vT%d" % h]][:, b * P : (b + 1) * P],
+                        in_=bank_of("vT%d" % h, i)[:, b * P : (b + 1) * P],
                         func=COPY,
-                        scale=sgn[:, j : j + 1],
+                        scale=(sgn_fifth if i in SUM_ON_TENSOR and i not in W_ON_VECTOR else sgn)[:, j : j + 1],
                     )
             elif kind == "k":
                 for j in range(4 * h, 4 * h + 4):
@@ -279,21 +329,16 @@ def tile_unrolledoverrelaxedadmmlasso_d2p_kernel(
                         scalar1=hi[:, j : j + 1], scalar2=lo[:, j : j + 1], op0=ALU.min, op1=ALU.max,
                     )
             elif kind == "b":
-                turn_blocks(at(ut, i), banks[BANK["uT%d" % h]], h)
+                turn_blocks(at(ut, i), bank_of("uT%d" % h, i, bank_id), h)
             elif kind == "o":
-                nc.scalar.copy(out=at(u1, i)[:, half(h)], in_=banks[BANK["uT%d" % h]][:])
+                nc.scalar.copy(out=at(u1, i)[:, half(h)], in_=bank_of("uT%d" % h, i)[:])
                 nc.sync.dma_start(out=out_1[rows_i, half(h)], in_=at(u1, i)[:, half(h)])
             elif kind == "z":
-                dual = banks[BANK["uT%d" % h]][:] if Z_FROM_PSUM else at(u1, i)[:, half(h)]
+                dual = bank_of("uT%d" % h, i)[:] if Z_FROM_PSUM else at(u1, i)[:, half(h)]
                 nc.vector.tensor_tensor(
                     out=at(z1, i)[:, half(h)], in0=at(v, i)[:, half(h)], in1=dual, op=ALU.subtract
                 )
                 nc.sync.dma_start(out=out_0[rows_i, half(h)], in_=at(z1, i)[:, half(h)])
 
-        for name, i in PRE:
-            stage(name, i)
-        for step in range(TILES + max(lag for name, lag in ORDER)):
-            for name, lag in ORDER:
-                i = step - lag
-                if 0 <= i < TILES and (name, i) not in PRE:
-                    stage(name, i)
+        for name, i, bank_id in SEQ:
+            stage(name, i, bank_id)

from contextlib import ExitStack

import concourse.mybir as mybir
from concourse.masks import make_identity

F32 = mybir.dt.float32
BF16 = mybir.dt.bfloat16
I32 = mybir.dt.int32
U32 = mybir.dt.uint32
U8 = mybir.dt.uint8
FP8 = mybir.dt.float8_e4m3fn
FP8X4 = mybir.dt.float8_e4m3fn_x4
FP4X4 = mybir.dt.float4_e2m1fn_x4
ALU = mybir.AluOpType
ACT = mybir.ActivationFunctionType
COPY = ACT.Copy

N, M, K = 1024, 1024, 1024
FLOPS = 2 * N * M * K + 2 * N * K * K
P = 128
TILES = N // P
HALF = 512
PASSES = 2

SEQ = [("widen", 0, -1), ("yT", 0, 0), ("c1", 0, -1), ("d", 0, -1), ("yc", 0, -1), ("qy", 0, -1), ("c0", 0, -1), ("C0a", 0, 1), ("q0", 0, 2), ("C0", 0, -1), ("c1", 1, -1), ("C1a", 0, 3), ("widen", 1, -1), ("s0", 0, -1), ("d", 1, -1), ("q1", 0, 4), ("C1", 0, -1), ("yT", 1, 5), ("widen", 2, -1), ("s1", 0, -1), ("W0", 2, 6), ("c0", 1, -1), ("W1", 2, 7), ("r", 0, -1), ("yc", 1, -1), ("yT", 2, 0), ("widen", 3, -1), ("qy", 1, -1), ("rT", 0, 1), ("d", 2, -1), ("q1", 1, 2), ("yc", 2, -1), ("d", 3, -1), ("rc", 0, -1), ("yT", 3, 3), ("c1", 2, -1), ("q0", 1, 4), ("qr", 0, -1), ("yc", 3, -1), ("s1", 1, -1), ("x1", 0, 5), ("c0", 2, -1), ("s0", 1, -1), ("x0", 0, 0), ("widen", 4, -1), ("v1", 0, -1), ("W0", 5, 1), ("qy", 3, -1), ("t1", 0, 7), ("qy", 2, -1), ("widen", 5, -1), ("yT", 4, 3), ("r", 1, -1), ("q1", 2, 2), ("v0", 0, -1), ("e1", 0, -1), ("q0", 2, 6), ("s1", 2, -1), ("widen", 7, -1), ("t0", 0, 4), ("rT", 1, 5), ("s0", 2, -1), ("k1", 0, -1), ("W1", 4, 0), ("r", 2, -1), ("e0", 0, -1), ("b1", 0, 7), ("W1", 7, 2), ("c1", 4, -1), ("k0", 0, -1), ("o1", 0, -1), ("rT", 2, 6), ("d", 5, -1), ("b0", 0, 4), ("rc", 1, -1), ("q1", 3, 0), ("rc", 2, -1), ("z1", 0, -1), ("yc", 4, -1), ("yT", 5, 7), ("s1", 3, -1), ("o0", 0, -1), ("q0", 3, 5), ("qr", 2, -1), ("qr", 1, -1), ("yc", 5, -1), ("x0", 2, 6), ("z0", 0, -1), ("widen", 6, -1), ("x0", 1, 3), ("s0", 3, -1), ("x1", 1, 0), ("v0", 2, -1), ("x1", 2, 4), ("v0", 1, -1), ("r", 3, -1), ("yT", 6, 7), ("t0", 1, 5), ("yc", 6, -1), ("W1", 6, 6), ("v1", 2, -1), ("c0", 5, -1), ("rT", 3, 3), ("v1", 1, -1), ("e0", 1, -1), ("t1", 2, 7), ("qy", 6, -1), ("t1", 1, 4), ("qy", 4, -1), ("rc", 3, -1), ("d", 4, -1), ("q1", 6, 1), ("e1", 1, -1), ("q1", 4, 0), ("qr", 3, -1), ("c1", 6, -1), ("q0", 4, 5), ("k1", 1, -1), ("e1", 2, -1), ("s1", 4, -1), ("x1", 3, 3), ("x0", 3, 4), ("s0", 4, -1), ("v1", 3, -1), ("q0", 6, 6), ("k1", 2, -1), ("v0", 3, -1), ("r", 4, -1), ("b1", 1, 0), ("t0", 3, 7), ("o1", 1, -1), ("qy", 5, -1), ("k0", 1, -1), ("rT", 4, 5), ("z1", 1, -1), ("y0", 3, -1), ("b0", 1, 3), ("d", 6, -1), ("rc", 4, -1), ("q1", 5, 4), ("o0", 1, -1), ("q0", 5, 0), ("qr", 4, -1), ("e0", 3, -1), ("s1", 5, -1), ("x1", 4, 5), ("s0", 5, -1), ("W0", 4, 3), ("k0", 3, -1), ("t1", 3, 4), ("r", 5, -1), ("c0", 4, -1), ("b0", 3, 7), ("s0", 6, -1), ("y1", 3, -1), ("a0", 3, 0), ("s1", 6, -1), ("c1", 7, -1), ("W1", 5, 3), ("v1", 4, -1), ("z0", 3, -1), ("W0", 6, 6), ("r", 6, -1), ("c1", 5, -1), ("yT", 7, 1), ("e1", 3, -1), ("t1", 4, 2), ("d", 7, -1), ("t0", 2, 5), ("yc", 7, -1), ("rT", 5, 0), ("c0", 6, -1), ("qy", 7, -1), ("W0", 7, 3), ("z0", 1, -1), ("e1", 4, -1), ("q1", 7, 4), ("k1", 3, -1), ("c0", 7, -1), ("q0", 7, 1), ("k1", 4, -1), ("s1", 7, -1), ("e0", 2, -1), ("b1", 4, 6), ("s0", 7, -1), ("b1", 3, 2), ("rc", 5, -1), ("b1", 2, 3), ("k0", 2, -1), ("o1", 4, -1), ("x0", 4, 4), ("qr", 5, -1), ("r", 7, -1), ("o1", 3, -1), ("x0", 5, 5), ("o1", 2, -1), ("x1", 5, 1), ("v0", 4, -1), ("o0", 3, -1), ("b0", 2, 0), ("z1", 4, -1), ("t0", 4, 6), ("o0", 2, -1), ("rT", 7, 2), ("v0", 5, -1), ("e0", 4, -1), ("rT", 6, 3), ("z0", 2, -1), ("t0", 5, 4), ("v1", 5, -1), ("rc", 6, -1), ("a1", 3, 7), ("k0", 4, -1), ("rc", 7, -1), ("t1", 5, 0), ("qr", 6, -1), ("b0", 4, 5), ("z1", 2, -1), ("e0", 5, -1), ("x0", 6, 6), ("qr", 7, -1), ("e1", 5, -1), ("k0", 5, -1), ("x1", 7, 1), ("v0", 6, -1), ("z1", 3, -1), ("b0", 5, 3), ("v1", 7, -1), ("o0", 4, -1), ("t0", 6, 2), ("k1", 5, -1), ("x0", 7, 4), ("e0", 6, -1), ("z0", 4, -1), ("b1", 5, 0), ("v0", 7, -1), ("o0", 5, -1), ("t1", 7, 6), ("k0", 6, -1), ("o1", 5, -1), ("x1", 6, 7), ("z0", 5, -1), ("e1", 7, -1), ("b0", 6, 1), ("z1", 5, -1), ("t0", 7, 5), ("o0", 6, -1), ("k1", 7, -1), ("v1", 6, -1), ("e0", 7, -1), ("b1", 7, 2), ("z0", 6, -1), ("t1", 6, 4), ("o1", 7, -1), ("k0", 7, -1), ("e1", 6, -1), ("z1", 7, -1), ("b0", 7, 3), ("o0", 7, -1), ("k1", 6, -1), ("b1", 6, 0), ("z0", 7, -1), ("o1", 6, -1), ("z1", 6, -1)]
DEPTH = {"ybf":3,"yg":3,"yq":3,"ys":3,"d":4,"s":3,"rb":3,"rg":3,"rq":3,"rs":3,"w":4,"v":5,"vt":3,"ut":3,"u1":5,"z1":5,"nv":1}
D_ON_GPSIMD = []
W_ON_VECTOR = [0,1]
WIDEN_ON_VECTOR = [0]
SUM_ON_TENSOR = [3]
Z_FROM_PSUM = False


def tile_unrolledoverrelaxedadmmlasso_d2p_kernel(
    tc, y_bytes, y_scale, a_words, a_scales, g, minv_words, minv_scales, z0, u0, lam, out_0, out_1
):
    nc = tc.nc
    with ExitStack() as ctx:
        keep = ctx.enter_context(tc.tile_pool(name="keep", bufs=1))
        psum = ctx.enter_context(tc.psum_pool(name="psum", bufs=1))
        ctx.enter_context(tc.manual_schedule())

        def ring(name, width, dtype):
            return [
                keep.tile([P, width], dtype, name="%s_%d" % (name, j), align_bytes=64) for j in range(DEPTH[name])
            ]

        banks = [psum.tile([P, HALF], F32, name="bank_%d" % j) for j in range(8)]
        held = {}

        def bank_of(role, i, fresh=None):
            if fresh is not None:
                held[role, i] = banks[fresh]
            return held[role, i]

        y_raw = keep.tile([P, TILES, M], U8, name="y_raw", align_bytes=64)
        y_sc = keep.tile([P, TILES * TILES], F32, name="y_sc", align_bytes=64)
        z_sb = keep.tile([P, TILES, K], BF16, name="z_sb", align_bytes=64)
        u_sb = keep.tile([P, TILES, K], BF16, name="u_sb", align_bytes=64)
        a_sb = keep.tile([P, PASSES, 2 * K], U8, name="a_sb", align_bytes=64)
        m_sb = keep.tile([P, PASSES, 2 * K], U8, name="m_sb", align_bytes=64)
        a_pl = keep.tile([P, PASSES, K], U8, name="a_pl", align_bytes=64)
        m_pl = keep.tile([P, PASSES, K], U8, name="m_pl", align_bytes=64)
        ident_f = keep.tile([P, P], F32, name="ident_f", align_bytes=64)
        ident_b = keep.tile([P, P], BF16, name="ident_b", align_bytes=64)
        diag_u = keep.tile([P, P], BF16, name="diag_u", align_bytes=64)
        diag_z = keep.tile([P, P], BF16, name="diag_z", align_bytes=64)
        rows = keep.tile([P, P], BF16, name="rows", align_bytes=64)
        cols = keep.tile([P, 8], BF16, name="cols", align_bytes=64)
        hi = keep.tile([P, 8], F32, name="hi", align_bytes=64)
        lo = keep.tile([P, 8], F32, name="lo", align_bytes=64)
        sgn_fifth = keep.tile([P, 8], F32, name="sgn_fifth", align_bytes=64)
        sgn = keep.tile([P, 8], F32, name="sgn", align_bytes=64)
        g_all = keep.tile([P, K], BF16, name="g_all", align_bytes=64)
        warm = keep.tile([P, 8], F32, name="warm", align_bytes=64)

        ybf = ring("ybf", M, BF16)
        yg = ring("yg", M, BF16)
        yq = ring("yq", M // 4, U32)
        ys = ring("ys", M // 4, U8)
        d = ring("d", K, F32)
        s = ring("s", K, F32)
        rb = ring("rb", K, BF16)
        rg = ring("rg", K, BF16)
        rq = ring("rq", K // 4, U32)
        rs = ring("rs", K // 4, U8)
        w = ring("w", K, F32)
        v = ring("v", K, F32)
        vt = ring("vt", K, F32)
        ut = ring("ut", K, F32)
        u1 = ring("u1", K, F32)
        z1 = ring("z1", K, F32)
        nv = ring("nv", K, F32)

        def at(tiles, i):
            return tiles[i % len(tiles)]

        def load_rows(dst, src, first, count):
            nc.sync.dma_start(
                out=dst[:, first : first + count, :],
                in_=src[first * P : (first + count) * P, :].rearrange("(t p) k -> p t k", p=P),
            )

        def load_words(dst, src):
            nc.sync.dma_start(out=dst[:].bitcast(I32), in_=src.rearrange("g p n -> p g n").bitcast(I32))

        def load_plane(queue, dst, src):
            for q in range(4):
                queue.dma_start(
                    out=dst[32 * q : 32 * q + 4, :, :].bitcast(I32),
                    in_=src[:, 4 * q : 4 * q + 4, :].rearrange("g r n -> r g n").bitcast(I32),
                )

        nc.vector.memset(warm[:], 0.0)
        nc.vector.memset(a_pl[:].bitcast(I32), 0)
        nc.vector.memset(rows[:], 0.0)
        nc.vector.memset(m_pl[:].bitcast(I32), 0)
        make_identity(nc, ident_f[:])
        nc.scalar.activation(out=warm[:, 4:5], in_=warm[:, 0:1], func=ACT.Sign)
        nc.vector.tensor_copy(out=ident_b[:], in_=ident_f[:])
        nc.vector.tensor_scalar(out=diag_u[:], in0=ident_f[:], scalar1=5.0, scalar2=None, op0=ALU.mult)
        nc.vector.tensor_scalar(out=diag_z[:], in0=ident_f[:], scalar1=-3.0, scalar2=None, op0=ALU.mult)

        load_rows(y_raw, y_bytes, 0, 1)
        nc.sync.dma_start(out=y_sc[:], in_=y_scale.rearrange("a b -> (a b)").partition_broadcast(P))
        load_rows(z_sb, z0, 0, 1)
        load_rows(u_sb, u0, 0, 1)
        load_plane(nc.sync, a_pl, a_scales)
        load_words(a_sb, a_words)
        nc.sync.dma_start(out=rows[0:8, :], in_=lam.rearrange("(b p) -> b p", p=P))
        nc.sync.dma_start(out=rows[8:16, :], in_=g.rearrange("(b p) -> b p", p=P))
        load_rows(z_sb, z0, 1, 1)
        load_rows(u_sb, u0, 1, 1)
        load_rows(y_raw, y_bytes, 1, 1)
        load_rows(y_raw, y_bytes, 2, 2)
        load_rows(z_sb, z0, 2, 1)
        load_rows(u_sb, u0, 2, 1)
        load_plane(nc.sync, m_pl, minv_scales)
        load_words(m_sb, minv_words)
        load_rows(z_sb, z0, 3, 1)
        load_rows(u_sb, u0, 3, 1)
        load_rows(y_raw, y_bytes, 4, 4)
        load_rows(z_sb, z0, 4, 2)
        load_rows(u_sb, u0, 4, 2)
        load_rows(z_sb, z0, 6, 2)
        load_rows(u_sb, u0, 6, 2)

        def columns(i):
            view = bank_of("c", 0)[:].bitcast(BF16)
            nc.scalar.copy(out=cols[:], in_=view[:, 8:16])
            nc.scalar.activation(out=sgn[:], in_=view[:, 0:8], func=ACT.Sign)
            nc.scalar.activation(out=hi[:], in_=view[:, 0:8], func=ACT.Abs, scale=1.25)
            nc.scalar.activation(out=lo[:], in_=hi[:], func=COPY, scale=-1.0)
            nc.scalar.activation(out=sgn_fifth[:], in_=sgn[:], func=COPY, scale=0.2)

        def spread_gain(bank_id):
            view = bank_of("c", 1, bank_id)[:].bitcast(BF16)
            for b in range(8):
                nc.tensor.transpose(
                    view[:, b * P : (b + 1) * P], cols[:, b : b + 1].to_broadcast([P, P]), ident_b[:]
                )

        def widen(i):
            for j in range(TILES):
                dst = at(ybf, i)[:, j * P : (j + 1) * P]
                src = y_raw[:, i, j * P : (j + 1) * P].bitcast(FP8)
                scale = y_sc[:, i * TILES + j : i * TILES + j + 1]
                if i in WIDEN_ON_VECTOR:
                    nc.vector.tensor_scalar(out=dst, in0=src, scalar1=scale, scalar2=None, op0=ALU.mult)
                else:
                    nc.scalar.activation(out=dst, in_=src, func=COPY, scale=scale)

        def turn_words(src, bank):
            words = src[:].bitcast(F32)
            for c in range(PASSES):
                for e in range(2):
                    nc.tensor.transpose(
                        bank[:, (2 * c + e) * P : (2 * c + e + 1) * P],
                        words[:, 256 * c + e : 256 * (c + 1) : 2],
                        ident_f[:],
                    )

        def group_words(bank, dst):
            nc.scalar.copy(
                out=dst[:].bitcast(F32).rearrange("p (c r e) -> p c r e", c=PASSES, e=2),
                in_=bank[:].rearrange("p (c e r) -> p c r e", c=PASSES, e=2),
            )

        def quantize(src, codes, scales):
            nc.vector.quantize_mx(out=codes[:].bitcast(FP8X4), scales=scales[:], in_=src[:])

        def product(bank, codes, scales, words, plane, h):
            for c in range(PASSES):
                nc.tensor.matmul_mx(
                    out=bank[:],
                    lhsT=codes[:, c * P : (c + 1) * P].bitcast(FP8X4),
                    lhsT_scale=scales[:, c * P : (c + 1) * P],
                    rhs=words[:, c, 2 * HALF * h : 2 * HALF * (h + 1)].bitcast(FP4X4),
                    rhs_scale=plane[:, c, HALF * h : HALF * (h + 1)],
                    start=(c == 0),
                    stop=(c == PASSES - 1),
                )

        def half(h):
            return slice(HALF * h, HALF * (h + 1))

        def turn_blocks(src, bank, h):
            for b in range(4):
                nc.tensor.transpose(
                    bank[:, b * P : (b + 1) * P], src[:, HALF * h + b * P : HALF * h + (b + 1) * P], ident_f[:]
                )

        def stage(name, i, bank_id):
            kind = name[0]
            h = int(name[1]) if name[1:] in ("0", "1") else 0
            rows_i = slice(i * P, (i + 1) * P)
            if name == "C0":
                columns(i)
            elif name == "C0a":
                nc.tensor.transpose(bank_of("c", 0, bank_id)[:].bitcast(BF16)[:, 0:P], rows[:], ident_b[:])
            elif name == "C1a":
                spread_gain(bank_id)
            elif name == "C1":
                nc.scalar.copy(out=g_all[:], in_=bank_of("c", 1)[:].bitcast(BF16))
            elif name == "widen":
                widen(i)
            elif name == "yT":
                turn_words(at(ybf, i), bank_of("yT0", i, bank_id))
            elif name == "yc":
                group_words(bank_of("yT0", i), at(yg, i))
            elif name == "qy":
                quantize(at(yg, i), at(yq, i), at(ys, i))
            elif name == "d":
                eng = nc.gpsimd if i in D_ON_GPSIMD else nc.vector
                eng.tensor_tensor(out=at(d, i)[:], in0=z_sb[:, i, :], in1=u_sb[:, i, :], op=ALU.subtract)
            elif name == "r":
                nc.vector.tensor_tensor(out=at(rb, i)[:], in0=at(s, i)[:], in1=g_all[:], op=ALU.mult)
            elif name == "rT":
                turn_words(at(rb, i), bank_of("rT0", i, bank_id))
            elif name == "rc":
                group_words(bank_of("rT0", i), at(rg, i))
            elif name == "qr":
                quantize(at(rg, i), at(rq, i), at(rs, i))
            elif kind == "q":
                product(bank_of("q%d" % h, i, bank_id), at(yq, i), at(ys, i), a_sb, a_pl, h)
            elif kind == "s":
                nc.vector.scalar_tensor_tensor(
                    out=at(s, i)[:, half(h)], in0=at(d, i)[:, half(h)], scalar=0.8,
                    in1=bank_of("q%d" % h, i)[:], op0=ALU.mult, op1=ALU.add,
                )
            elif kind == "W":
                if i not in W_ON_VECTOR and i not in SUM_ON_TENSOR:
                    bank = bank_of("W%d" % h, i, bank_id)
                    nc.tensor.matmul(bank[:], lhsT=diag_u[:], rhs=u_sb[:, i, half(h)], start=True, stop=False)
                    nc.tensor.matmul(bank[:], lhsT=diag_z[:], rhs=z_sb[:, i, half(h)], start=False, stop=True)
            elif kind == "c":
                if i not in W_ON_VECTOR:
                    nc.scalar.activation(
                        out=at(w, i)[:, half(h)], in_=bank_of("W%d" % h, i)[:], func=COPY, scale=0.2
                    )
                else:
                    nc.vector.scalar_tensor_tensor(
                        out=at(w, i)[:, half(h)], in0=z_sb[:, i, half(h)], scalar=-0.6,
                        in1=u_sb[:, i, half(h)], op0=ALU.mult, op1=ALU.add,
                    )
            elif kind == "x":
                product(bank_of("x%d" % h, i, bank_id), at(rq, i), at(rs, i), m_sb, m_pl, h)
            elif kind == "v" and i in SUM_ON_TENSOR:
                nc.scalar.activation(
                    out=at(v, i)[:, half(h)], in_=bank_of("x%d" % h, i)[:], func=COPY,
                    scale=1.6 if i in W_ON_VECTOR else 8.0,
                )
            elif kind == "t" and i in SUM_ON_TENSOR:
                bank = bank_of("vT%d" % h, i, bank_id)
                for b in range(4):
                    blk = slice(HALF * h + b * P, HALF * h + (b + 1) * P)
                    dst = bank[:, b * P : (b + 1) * P]
                    nc.tensor.matmul(
                        dst, lhsT=at(v, i)[:, blk], rhs=ident_f[:], is_transpose=True, start=True, stop=False
                    )
                    if i in W_ON_VECTOR:
                        nc.tensor.matmul(
                            dst, lhsT=at(w, i)[:, blk], rhs=ident_f[:], is_transpose=True, start=False, stop=True
                        )
                    else:
                        nc.tensor.matmul(dst, lhsT=u_sb[:, i, blk], rhs=diag_u[:], start=False, stop=False)
                        nc.tensor.matmul(dst, lhsT=z_sb[:, i, blk], rhs=diag_z[:], start=False, stop=True)
            elif kind == "y":
                nc.scalar.activation(
                    out=at(nv, i)[:, half(h)], in_=bank_of("vT%d" % h, i)[:], func=COPY,
                    scale=-1.0 if i in W_ON_VECTOR else -0.2,
                )
            elif kind == "a":
                bank = bank_of("zT%d" % h, i, bank_id)
                for b in range(4):
                    blk = slice(HALF * h + b * P, HALF * h + (b + 1) * P)
                    dst = bank[:, b * P : (b + 1) * P]
                    nc.tensor.matmul(
                        dst, lhsT=at(ut, i)[:, blk], rhs=ident_f[:], is_transpose=True, start=True, stop=False
                    )
                    nc.tensor.matmul(
                        dst, lhsT=at(nv, i)[:, blk], rhs=ident_f[:], is_transpose=True, start=False, stop=True
                    )
            elif kind == "z" and i in SUM_ON_TENSOR:
                nc.scalar.activation(
                    out=at(z1, i)[:, half(h)], in_=bank_of("zT%d" % h, i)[:], func=COPY, scale=-1.0
                )
                nc.sync.dma_start(out=out_0[rows_i, half(h)], in_=at(z1, i)[:, half(h)])
            elif kind == "v":
                nc.vector.scalar_tensor_tensor(
                    out=at(v, i)[:, half(h)], in0=bank_of("x%d" % h, i)[:], scalar=1.6,
                    in1=at(w, i)[:, half(h)], op0=ALU.mult, op1=ALU.add,
                )
            elif kind == "t":
                turn_blocks(at(v, i), bank_of("vT%d" % h, i, bank_id), h)
            elif kind == "e":
                for b in range(4):
                    j = 4 * h + b
                    nc.scalar.activation(
                        out=at(vt, i)[:, j * P : (j + 1) * P],
                        in_=bank_of("vT%d" % h, i)[:, b * P : (b + 1) * P],
                        func=COPY,
                        scale=(sgn_fifth if i in SUM_ON_TENSOR and i not in W_ON_VECTOR else sgn)[:, j : j + 1],
                    )
            elif kind == "k":
                for j in range(4 * h, 4 * h + 4):
                    nc.vector.tensor_scalar(
                        out=at(ut, i)[:, j * P : (j + 1) * P], in0=at(vt, i)[:, j * P : (j + 1) * P],
                        scalar1=hi[:, j : j + 1], scalar2=lo[:, j : j + 1], op0=ALU.min, op1=ALU.max,
                    )
            elif kind == "b":
                turn_blocks(at(ut, i), bank_of("uT%d" % h, i, bank_id), h)
            elif kind == "o":
                nc.scalar.copy(out=at(u1, i)[:, half(h)], in_=bank_of("uT%d" % h, i)[:])
                nc.sync.dma_start(out=out_1[rows_i, half(h)], in_=at(u1, i)[:, half(h)])
            elif kind == "z":
                dual = bank_of("uT%d" % h, i)[:] if Z_FROM_PSUM else at(u1, i)[:, half(h)]
                nc.vector.tensor_tensor(
                    out=at(z1, i)[:, half(h)], in0=at(v, i)[:, half(h)], in1=dual, op=ALU.subtract
                )
                nc.sync.dma_start(out=out_0[rows_i, half(h)], in_=at(z1, i)[:, half(h)])

        for name, i, bank_id in SEQ:
            stage(name, i, bank_id)
